import numpy as np
CORES = [48,49,50,51,52,53,54,55,56,57,58,59,60,61,62,63]
N = 16
ROOT = 2
def setup_inputs(rng):
    return {"x": rng.standard_normal((N, 128, N * 256), dtype=np.float32)}
def reference(x):
    return {"y": np.stack([x[ROOT][:, r * 256:(r + 1) * 256] for r in range(N)])}

@@ -1,0 +1,133 @@
+import concourse.bass as bass
+
+B = 256
+ROOT = 50
+
+SCRATCH = {
+    "buf": ("sbuf", [128, 16 * B], "float32"),
+    "fw": ("sbuf", [128, 4 * B], "float32"),
+    "land": ("sbuf", [128, B], "float32"),
+}
+SEMAPHORES = ["own", "sent", "stored", "ld0", "ld1", "ld2", "ld3", "ld4", "ld5", "ld6", "ld7",
+              "grp0", "grp1", "grp2", "grp3"]
+
+
+def sem_table(T):
+    s = T.sem
+    return {"own": s.own, "sent": s.sent, "stored": s.stored, "ld0": s.ld0, "ld1": s.ld1, "ld2": s.ld2, "ld3": s.ld3,
+            "ld4": s.ld4, "ld5": s.ld5, "ld6": s.ld6, "ld7": s.ld7, "grp0": s.grp0, "grp1": s.grp1, "grp2": s.grp2,
+            "grp3": s.grp3}
+
+
+def rng_mask(lo, n):
+    return ((1 << n) - 1) << lo
+
+
+def own(r):
+    return 48 + r
+
+
+def root_ops():
+    c = own
+    return [
+        ("load", 12, 16),
+        ("load", 8, 12),
+        ("send", [(12, [54, c(12)], 0, 4), (13, [54, c(13)], 4, 4), (14, [55, c(14)], 8, 4), (15, [55, c(15)], 12, 4)]),
+        ("load", 4, 8),
+        ("send", [(8, [51, c(8)], 0, 4), (9, [51, c(9)], 4, 4), (10, [51, c(10)], 8, 4), (11, [51, c(11)], 12, 4)]),
+        ("load", 0, 4),
+        ("send", [(4, [c(4)], 0, 4), (5, [c(5)], 4, 4), (6, [c(6)], 8, 4), (7, [c(7)], 12, 4)]),
+        ("send", [(0, [c(0)], 0, 4), (1, [c(1)], 4, 4), (3, [c(3)], 8, 8)]),
+        ("own",),
+    ]
+
+
+def build(topo):
+    acts = {}
+    slots = {}
+    grps = {}
+
+    def add(core, a):
+        acts.setdefault(core, []).append(a)
+
+    def send(src, items):
+        trs = []
+        groups = {}
+        for slot, blk, way, mask in items:
+            nxt = way[0]
+            assert topo.may_write(src, nxt) and (mask & ~topo.mask(src, nxt)) == 0
+            n = bin(mask).count("1")
+            if len(way) == 1:
+                trs.append((slot, blk, nxt, None, "own", mask))
+                add(nxt, ("store", n))
+            else:
+                s = slots.get(nxt, 0)
+                slots[nxt] = s + 1
+                if nxt not in groups:
+                    k = grps.get(nxt, 0)
+                    grps[nxt] = k + 1
+                    groups[nxt] = ["grp%d" % k, 0, []]
+                gr = groups[nxt]
+                gr[1] += n
+                gr[2].append((s, blk, way[1:]))
+                trs.append((slot, blk, nxt, s, gr[0], mask))
+        add(src, ("call", trs))
+        for nxt, (sem, total, lst) in groups.items():
+            add(nxt, ("wait", sem, total))
+            width = 16 if all(topo.chip(it[2][0]) == topo.chip(nxt) for it in lst) else 8
+            per = 1
+            while per * 2 * len(lst) <= width:
+                per *= 2
+            send(nxt, [(it[0], it[1], it[2], rng_mask(i * per, per)) for i, it in enumerate(lst)])
+
+    loads = []
+    for op in root_ops():
+        if op[0] == "load":
+            sem = "ld%d" % len(loads)
+            loads.append([op[1], op[2], sem, False])
+            add(ROOT, ("load", op[1], op[2], sem))
+        elif op[0] == "send":
+            for ld in loads:
+                if not ld[3] and any(ld[0] <= it[0] < ld[1] for it in op[1]):
+                    ld[3] = True
+                    add(ROOT, ("wait", ld[2], 16))
+            send(ROOT, [(None, b, w, rng_mask(lo, n)) for b, w, lo, n in op[1]])
+        else:
+            add(ROOT, ("own",))
+    return acts
+
+
+def rank_program(g, core, T, topo):
+    acts = build(topo).get(core)
+    if not acts:
+        return
+    sem = sem_table(T)
+    sent = 0
+    stored = 0
+    for a in acts:
+        if a[0] == "load":
+            g.dma_start(T.buf[:, a[1] * B:a[2] * B], T.x[:, a[1] * B:a[2] * B]).then_inc(sem[a[3]], 16)
+        elif a[0] == "wait":
+            g.wait_ge(sem[a[1]], a[2])
+        elif a[0] == "own":
+            r = T.rank_of(core)
+            g.dma_start(T.y[:], T.x[:, r * B:(r + 1) * B]).then_inc(sem["stored"], 16)
+            stored += 16
+        elif a[0] == "store":
+            g.wait_ge(sem["own"], a[1])
+            g.dma_start(T.y[:], T.land[:]).then_inc(sem["stored"], 16)
+            stored += 16
+        else:
+            trs = []
+            for slot, blk, nxt, dslot, sname, mask in a[1]:
+                src = T.buf[:, blk * B:(blk + 1) * B] if slot is None else T.fw[:, slot * B:(slot + 1) * B]
+                dst = T.land[:] if dslot is None else T.fw[:, dslot * B:(dslot + 1) * B]
+                rid, pid, se = topo.addr(nxt)
+                trs.append(bass.RemoteDMATransfer(dst_ids=[bass.DstId(rid=rid, pnc=pid)], dma_engine_mask=mask,
+                                                  remote_sem=sem[sname], src=src, dst=dst))
+                sent += bin(mask).count("1")
+            g.remote_dma_fused(trs, local_sem=sem["sent"])
+    if sent:
+        g.wait_ge(sem["sent"], sent)
+    if stored:
+        g.wait_ge(sem["stored"], stored)

@@ -29,12 +29,20 @@ def own(r):
 
 def root_ops():
     c = own
+
+    def pair(b, d0):
+        return ("send", [(b, [51, c(b)], 0, 8), (b + 1, [d0, c(b + 1)], 8, 8)])
+
     return [
-        ("load", 12, 16),
-        ("load", 8, 12),
-        ("send", [(12, [54, c(12)], 0, 4), (13, [54, c(13)], 4, 4), (14, [55, c(14)], 8, 4), (15, [55, c(15)], 12, 4)]),
+        ("load", 8, 10),
+        ("load", 10, 12),
+        pair(8, 54),
+        ("load", 12, 14),
+        pair(10, 55),
+        ("load", 14, 16),
+        pair(12, 54),
         ("load", 4, 8),
-        ("send", [(8, [51, c(8)], 0, 4), (9, [51, c(9)], 4, 4), (10, [51, c(10)], 8, 4), (11, [51, c(11)], 12, 4)]),
+        pair(14, 55),
         ("load", 0, 4),
         ("send", [(4, [c(4)], 0, 4), (5, [c(5)], 4, 4), (6, [c(6)], 8, 4), (7, [c(7)], 12, 4)]),
         ("send", [(0, [c(0)], 0, 4), (1, [c(1)], 4, 4), (3, [c(3)], 8, 8)]),

@@ -29,21 +29,14 @@ def own(r):
 
 def root_ops():
     c = own
-
-    def pair(b, d0):
-        return ("send", [(b, [51, c(b)], 0, 8), (b + 1, [d0, c(b + 1)], 8, 8)])
-
     return [
-        ("load", 8, 10),
-        ("load", 10, 12),
-        pair(8, 54),
-        ("load", 12, 14),
-        pair(10, 55),
-        ("load", 14, 16),
-        pair(12, 54),
+        ("load", 8, 12),
+        ("load", 12, 16),
+        ("send", [(8, [49, 34, c(8)], 0, 4), (9, [53, 38, c(9)], 4, 4), (10, [51, c(10)], 8, 4), (11, [54, c(11)], 12, 4)]),
+        ("send", [(12, [51, c(12)], 0, 4), (13, [51, c(13)], 4, 4), (14, [54, c(14)], 8, 4), (15, [55, c(15)], 12, 4)]),
         ("load", 4, 8),
-        pair(14, 55),
-        ("load", 0, 4),
+        ("load", 0, 2),
+        ("load", 3, 4),
         ("send", [(4, [c(4)], 0, 4), (5, [c(5)], 4, 4), (6, [c(6)], 8, 4), (7, [c(7)], 12, 4)]),
         ("send", [(0, [c(0)], 0, 4), (1, [c(1)], 4, 4), (3, [c(3)], 8, 8)]),
         ("own",),

@@ -34,11 +34,11 @@ def root_ops():
         ("load", 12, 16),
         ("send", [(8, [49, 34, c(8)], 0, 4), (9, [53, 38, c(9)], 4, 4), (10, [51, c(10)], 8, 4), (11, [54, c(11)], 12, 4)]),
         ("send", [(12, [51, c(12)], 0, 4), (13, [51, c(13)], 4, 4), (14, [54, c(14)], 8, 4), (15, [55, c(15)], 12, 4)]),
-        ("load", 4, 8),
         ("load", 0, 2),
-        ("load", 3, 4),
+        ("load", 3, 8),
+        ("send", [(0, [c(0)], 0, 8), (1, [c(1)], 8, 8)]),
         ("send", [(4, [c(4)], 0, 4), (5, [c(5)], 4, 4), (6, [c(6)], 8, 4), (7, [c(7)], 12, 4)]),
-        ("send", [(0, [c(0)], 0, 4), (1, [c(1)], 4, 4), (3, [c(3)], 8, 8)]),
+        ("send", [(3, [c(3)], 0, 16)]),
         ("own",),
     ]
 

@@ -32,8 +32,8 @@ def root_ops():
     return [
         ("load", 8, 12),
         ("load", 12, 16),
-        ("send", [(8, [49, 34, c(8)], 0, 4), (9, [53, 38, c(9)], 4, 4), (10, [51, c(10)], 8, 4), (11, [54, c(11)], 12, 4)]),
-        ("send", [(12, [51, c(12)], 0, 4), (13, [51, c(13)], 4, 4), (14, [54, c(14)], 8, 4), (15, [55, c(15)], 12, 4)]),
+        ("send", [(8, [34, c(8)], 0, 4), (9, [c(9)], 4, 4), (10, [54, c(10)], 8, 4), (11, [55, c(11)], 12, 4)]),
+        ("send", [(12, [35, c(12)], 0, 4), (13, [c(13)], 4, 4), (14, [51, c(14)], 8, 4), (15, [54, c(15)], 12, 4)]),
         ("load", 0, 2),
         ("load", 3, 8),
         ("send", [(0, [c(0)], 0, 8), (1, [c(1)], 8, 8)]),

import concourse.bass as bass

B = 256
ROOT = 50

SCRATCH = {
    "buf": ("sbuf", [128, 16 * B], "float32"),
    "fw": ("sbuf", [128, 4 * B], "float32"),
    "land": ("sbuf", [128, B], "float32"),
}
SEMAPHORES = ["own", "sent", "stored", "ld0", "ld1", "ld2", "ld3", "ld4", "ld5", "ld6", "ld7",
              "grp0", "grp1", "grp2", "grp3"]


def sem_table(T):
    s = T.sem
    return {"own": s.own, "sent": s.sent, "stored": s.stored, "ld0": s.ld0, "ld1": s.ld1, "ld2": s.ld2, "ld3": s.ld3,
            "ld4": s.ld4, "ld5": s.ld5, "ld6": s.ld6, "ld7": s.ld7, "grp0": s.grp0, "grp1": s.grp1, "grp2": s.grp2,
            "grp3": s.grp3}


def rng_mask(lo, n):
    return ((1 << n) - 1) << lo


def own(r):
    return 48 + r


def root_ops():
    c = own
    return [
        ("load", 8, 12),
        ("load", 12, 16),
        ("send", [(8, [34, c(8)], 0, 4), (9, [c(9)], 4, 4), (10, [54, c(10)], 8, 4), (11, [55, c(11)], 12, 4)]),
        ("send", [(12, [35, c(12)], 0, 4), (13, [c(13)], 4, 4), (14, [51, c(14)], 8, 4), (15, [54, c(15)], 12, 4)]),
        ("load", 0, 2),
        ("load", 3, 8),
        ("send", [(0, [c(0)], 0, 8), (1, [c(1)], 8, 8)]),
        ("send", [(4, [c(4)], 0, 4), (5, [c(5)], 4, 4), (6, [c(6)], 8, 4), (7, [c(7)], 12, 4)]),
        ("send", [(3, [c(3)], 0, 16)]),
        ("own",),
    ]


def build(topo):
    acts = {}
    slots = {}
    grps = {}

    def add(core, a):
        acts.setdefault(core, []).append(a)

    def send(src, items):
        trs = []
        groups = {}
        for slot, blk, way, mask in items:
            nxt = way[0]
            assert topo.may_write(src, nxt) and (mask & ~topo.mask(src, nxt)) == 0
            n = bin(mask).count("1")
            if len(way) == 1:
                trs.append((slot, blk, nxt, None, "own", mask))
                add(nxt, ("store", n))
            else:
                s = slots.get(nxt, 0)
                slots[nxt] = s + 1
                if nxt not in groups:
                    k = grps.get(nxt, 0)
                    grps[nxt] = k + 1
                    groups[nxt] = ["grp%d" % k, 0, []]
                gr = groups[nxt]
                gr[1] += n
                gr[2].append((s, blk, way[1:]))
                trs.append((slot, blk, nxt, s, gr[0], mask))
        add(src, ("call", trs))
        for nxt, (sem, total, lst) in groups.items():
            add(nxt, ("wait", sem, total))
            width = 16 if all(topo.chip(it[2][0]) == topo.chip(nxt) for it in lst) else 8
            per = 1
            while per * 2 * len(lst) <= width:
                per *= 2
            send(nxt, [(it[0], it[1], it[2], rng_mask(i * per, per)) for i, it in enumerate(lst)])

    loads = []
    for op in root_ops():
        if op[0] == "load":
            sem = "ld%d" % len(loads)
            loads.append([op[1], op[2], sem, False])
            add(ROOT, ("load", op[1], op[2], sem))
        elif op[0] == "send":
            for ld in loads:
                if not ld[3] and any(ld[0] <= it[0] < ld[1] for it in op[1]):
                    ld[3] = True
                    add(ROOT, ("wait", ld[2], 16))
            send(ROOT, [(None, b, w, rng_mask(lo, n)) for b, w, lo, n in op[1]])
        else:
            add(ROOT, ("own",))
    return acts


def rank_program(g, core, T, topo):
    acts = build(topo).get(core)
    if not acts:
        return
    sem = sem_table(T)
    sent = 0
    stored = 0
    for a in acts:
        if a[0] == "load":
            g.dma_start(T.buf[:, a[1] * B:a[2] * B], T.x[:, a[1] * B:a[2] * B]).then_inc(sem[a[3]], 16)
        elif a[0] == "wait":
            g.wait_ge(sem[a[1]], a[2])
        elif a[0] == "own":
            r = T.rank_of(core)
            g.dma_start(T.y[:], T.x[:, r * B:(r + 1) * B]).then_inc(sem["stored"], 16)
            stored += 16
        elif a[0] == "store":
            g.wait_ge(sem["own"], a[1])
            g.dma_start(T.y[:], T.land[:]).then_inc(sem["stored"], 16)
            stored += 16
        else:
            trs = []
            for slot, blk, nxt, dslot, sname, mask in a[1]:
                src = T.buf[:, blk * B:(blk + 1) * B] if slot is None else T.fw[:, slot * B:(slot + 1) * B]
                dst = T.land[:] if dslot is None else T.fw[:, dslot * B:(dslot + 1) * B]
                rid, pid, se = topo.addr(nxt)
                trs.append(bass.RemoteDMATransfer(dst_ids=[bass.DstId(rid=rid, pnc=pid)], dma_engine_mask=mask,
                                                  remote_sem=sem[sname], src=src, dst=dst))
                sent += bin(mask).count("1")
            g.remote_dma_fused(trs, local_sem=sem["sent"])
    if sent:
        g.wait_ge(sem["sent"], sent)
    if stored:
        g.wait_ge(sem["stored"], stored)
